import numpy as np
import ml_dtypes


def mxq(x, axis, fmt="e4m3"):
    dtype, down = {"e4m3": (ml_dtypes.float8_e4m3fn, 7), "e5m2": (ml_dtypes.float8_e5m2, 14)}[fmt]
    v = np.moveaxis(np.asarray(x, np.float32).astype(ml_dtypes.bfloat16).astype(np.float64), axis, -1)
    blocks = v.reshape(v.shape[:-1] + (-1, 32))
    amax = np.abs(blocks).max(-1, keepdims=True)
    byte = np.maximum(np.where(amax > 0, np.frexp(amax)[1] - 1 + 127, 0) - down, 1)
    scale = np.exp2(byte - 127.0)
    codes = (blocks / scale).astype(np.float32).astype(dtype).astype(np.float64)
    return np.moveaxis((codes * scale).reshape(v.shape), -1, axis)


WIDE = False


def mx_kscale(k):
    if not WIDE:
        return np.ones(k)
    levels = np.array([10, -10, 5, -5, 0])
    if k % 512:
        return np.exp2(np.random.permutation(np.resize(levels, k // 32))).repeat(32)
    a = np.empty((k // 512, 16))
    for p in range(k // 512):
        a[p, :8] = np.random.permutation(np.resize(levels, 8))
        for g in range(8):
            far = levels[np.abs(levels - a[p, g]) >= 10]
            a[p, g + 8] = far[np.random.randint(len(far))]
    return np.exp2(a.ravel()).repeat(32)


def f64(x):
    return np.asarray(x).astype(np.float64)


def striped(idx):
    return np.tile(idx.reshape(-1, 16).T, (8, 1)).astype(np.uint16)


def unstriped(offs):
    return offs[:16].T.reshape(-1).astype(np.int64)


def striped8(idx):
    return np.concatenate([x.reshape(-1, 16).T for x in idx]).astype(np.uint16)


def runs(offs, k):
    lists = np.stack([offs[16 * r : 16 * r + 16].T.reshape(-1) for r in range(8)]).astype(np.int64)
    return lists[np.arange(k) % 512 // 64]


def pack_weight(w):
    k, n = w.shape
    w = f64(np.asarray(w, np.float32).astype(ml_dtypes.bfloat16)).reshape(k // 32, 32, n)
    amax = np.abs(w).max(1)
    byte = np.clip(np.where(amax > 0, np.frexp(amax)[1] - 1 + 127 - 7, 1), 1, 254)
    scaled = (w * np.exp2(127.0 - byte)[:, None, :]).reshape(k, n).astype(np.float32)
    words = np.ascontiguousarray(scaled.reshape(k // 512, 128, 4, n).transpose(0, 1, 3, 2)).astype(ml_dtypes.float8_e4m3fn).view(np.uint8)
    return words, np.ascontiguousarray(byte.astype(np.uint8).reshape(k // 512, 16, n))


def unpack_weight(words, scales):
    g, p, n, _ = words.shape
    vals = np.ascontiguousarray(words).view(ml_dtypes.float8_e4m3fn).astype(np.float64) * np.repeat(np.exp2(scales.astype(np.float64) - 127.0), 8, axis=1)[..., None]
    return vals.transpose(0, 1, 3, 2).reshape(g * 512, n)


K, T, S, N, G, H, W = 512, 1024, 256, 512, 2048, 512, 128


def setup_inputs():
    n = np.random.standard_normal
    s = mx_kscale(K)[:, None]
    u = mx_kscale(K)
    packed_xT = pack_weight(n((K, T)) * s)
    packed_dT = pack_weight(n((K, G)) / s)
    perm = np.random.permutation(S)
    return {
        "x_words": packed_xT[0],
        "x_scales": packed_xT[1],
        "d_words": packed_dT[0],
        "d_scales": packed_dT[1],
        "gn": (np.random.uniform(0.5, 1.5, (H, 1)) * u[:, None]).astype(np.float32),
        "w1": (n((H, N)) / np.sqrt(H) / u[:, None]).astype(np.float32),
        "offs": striped(np.random.permutation(T)[:S]),
        "k1": striped8(np.random.randint(0, G, (8, H))),
        "two": striped(np.random.permutation(T)[:S]),
        "k2": striped8(np.random.randint(0, G, (8, H))),
        "hz": striped8(np.random.randint(0, T, (8, S))),
        "k3": striped8(np.random.randint(0, G, (8, H))),
        "n1": striped(np.random.permutation(S)),
        "n2": striped(np.random.permutation(S)),
        "n3": striped(perm[:W]),
        "n4": striped(perm[W:]),
    }


def reference(x_words, x_scales, d_words, d_scales, gn, w1, offs, k1, two, k2, hz, k3, n1, n2, n3, n4):
    d_k1 = unpack_weight(d_words, d_scales)[np.arange(K)[:, None], runs(k1, K)]
    xq = unpack_weight(x_words, x_scales)[:, unstriped(offs)]
    d_k2 = unpack_weight(d_words, d_scales)[np.arange(K)[:, None], runs(k2, K)]
    x_two = unpack_weight(x_words, x_scales)[:, unstriped(two)]
    d_k3 = unpack_weight(d_words, d_scales)[np.arange(K)[:, None], runs(k3, K)]
    x_hz = unpack_weight(x_words, x_scales)[np.arange(K)[:, None], runs(hz, K)]
    h = 0.0625 * (d_k1.T @ xq + d_k2.T @ x_two + d_k3.T @ x_hz)
    ds = np.zeros((H, S))
    ds[:, unstriped(n1)] = h
    ds2 = np.zeros((H, S))
    ds2[:, unstriped(n2)] = h
    z = f64(gn) * (ds - ds2)
    h2 = mxq(f64(w1), 0, "e4m3").T @ mxq(z, 0, "e4m3")
    pa = h2[:, unstriped(n3)]
    pb = h2[:, unstriped(n4)]
    rb = pa - pb
    ra = 0.75 * (pa + pb)
    ua = np.zeros((N, S))
    ua[:, unstriped(n3)] = ra
    out = ua.copy()
    out[:, unstriped(n4)] = rb
    return out

@@ -1,0 +1,249 @@
+from contextlib import ExitStack
+
+import concourse.mybir as mybir
+from concourse.masks import make_identity
+
+K, T, S, N, G, H, W = 512, 1024, 256, 512, 2048, 512, 128
+FLOPS = 3 * 2 * K * H * S + 2 * H * N * S
+
+F32 = mybir.dt.float32
+BF16 = mybir.dt.bfloat16
+I32 = mybir.dt.int32
+U32 = mybir.dt.uint32
+U16 = mybir.dt.uint16
+U8 = mybir.dt.uint8
+FP8X4 = mybir.dt.float8_e4m3fn_x4
+COPY = mybir.ActivationFunctionType.Copy
+ADD = mybir.AluOpType.add
+SUB = mybir.AluOpType.subtract
+MULT = mybir.AluOpType.mult
+
+P = 128
+HALF_S = S // 2
+HALF_H = H // 2
+
+
+def tile_picked_mtthznsndsubhaar_none_p_kernel(
+    tc, x_words, x_scales, d_words, d_scales, gn, w1, offs, k1, two, k2, hz, k3, n1, n2, n3, n4, out
+):
+    nc = tc.nc
+    with ExitStack() as ctx:
+        lists = ctx.enter_context(tc.tile_pool(name="lists", bufs=1))
+        sb = ctx.enter_context(tc.tile_pool(name="sb", bufs=1))
+        st = ctx.enter_context(tc.tile_pool(name="st", bufs=1))
+        ps = ctx.enter_context(tc.psum_pool(name="ps", bufs=1))
+
+        def load_list(name, ap):
+            t = lists.tile(list(ap.shape), U16, name=name)
+            nc.sync.dma_start(t[:], ap)
+            return t
+
+        def piece(lst, start, count):
+            return lst[:, start // 16 : (start + count) // 16]
+
+        d_sc = sb.tile([P, G], U8, name="d_sc", align_bytes=64)
+        x_sc = [st.tile([P, T], U8, name="x_sc0", align_bytes=64, offset=3008), sb.tile([P, T], U8, name="x_sc1", align_bytes=64)]
+        d_w = sb.tile([P, G], I32, name="d_w", align_bytes=64)
+        x_w = sb.tile([P, T], I32, name="x_w", align_bytes=64)
+        nc.gpsimd.dma_start(d_w[:], d_words[0].rearrange("p n t -> p (n t)").bitcast(I32))
+        nc.gpsimd.dma_start(x_w[:], x_words[0].rearrange("p n t -> p (n t)").bitcast(I32))
+        nc.sync.dma_start(d_sc[:].bitcast(I32), d_scales[0].bitcast(I32).unsqueeze(1).to_broadcast([16, 8, G // 4]))
+        l_k1 = load_list("l_k1", k1)
+        nc.sync.dma_start(x_sc[0][:].bitcast(I32), x_scales[0].bitcast(I32).unsqueeze(1).to_broadcast([16, 8, T // 4]))
+        l_offs = load_list("l_offs", offs)
+        l_k2 = load_list("l_k2", k2)
+        l_two = load_list("l_two", two)
+        l_k3 = load_list("l_k3", k3)
+        l_hz = load_list("l_hz", hz)
+        d_lists = (l_k1, l_k2, l_k3)
+        x_lists = (l_offs, l_two, l_hz)
+
+        gn_raw = sb.tile([P, 4], F32, name="gn_raw")
+        with nc.allow_non_contiguous_dma(reason="one gain a partition and row tile"):
+            nc.sync.dma_start(gn_raw[:], gn.rearrange("(u p) o -> p (u o)", p=P))
+        l_n1 = load_list("l_n1", n1)
+        l_n2 = load_list("l_n2", n2)
+        l_n3 = load_list("l_n3", n3)
+        l_n4 = load_list("l_n4", n4)
+        nc.sync.dma_start(x_sc[1][:].bitcast(I32), x_scales[0].bitcast(I32).unsqueeze(1).to_broadcast([16, 8, T // 4]))
+        gain = sb.tile([P, 4], F32, name="gain")
+        nc.scalar.activation(gain[:], gn_raw[:], COPY, scale=0.0625)
+
+        widths = (3 * HALF_H + 3 * HALF_S, 3 * HALF_S, 3 * HALF_H)
+        planes = []
+        for n, width in enumerate(widths):
+            pl = sb.tile([P, width], U8, name="plane%d" % n, align_bytes=64)
+            nc.gpsimd.memset(pl[:].bitcast(I32), 0)
+            planes.append(pl)
+        ident = sb.tile([P, P], F32, name="ident", align_bytes=64)
+        make_identity(nc, ident[:])
+
+        at_got = (6976, 7040, 7424)
+        at_w = 8192
+
+        def gather_bytes(n, parts, tag):
+            got = st.tile([P, widths[n] + (128 if n == 0 else 0)], U8, name="got%d" % n, align_bytes=64, offset=at_got[n])
+            at, res = 0, []
+            for src, lst, count in parts:
+                nc.vector.tensor_copy(got[:, at : at + count], src[:].indirect(lst))
+                res.append(planes[n][:, at : at + count])
+                at = at + count
+            for r in range(4):
+                nc.sync.dma_start(planes[n][r:P:32, :].bitcast(I32), got[8 * r : P : 32, : widths[n]].bitcast(I32))
+            return res
+
+        def d_parts(half):
+            return [(d_sc, piece(l, half * HALF_H, HALF_H), HALF_H) for l in d_lists]
+
+        def x_parts(half):
+            return [(x_sc[half], piece(l, half * HALF_S, HALF_S), HALF_S) for l in x_lists]
+
+        mixed = []
+        for a, b in zip(d_parts(0), x_parts(0)):
+            mixed.extend([a, b])
+        sc0 = gather_bytes(0, mixed, "got0")
+        d_scale = [sc0[0::2], None]
+        x_scale = [sc0[1::2], None]
+
+        d_code = [st.tile([P, 3, HALF_H], U32, name="d_code0", align_bytes=64, offset=0), None]
+
+        def gather_d(a, half):
+            nc.vector.tensor_copy(
+                d_code[half][:, a, :], d_w[:].bitcast(U32).indirect(piece(d_lists[a], half * HALF_H, HALF_H))
+            )
+
+        x_code = [st.tile([P, 3, HALF_S], U32, name="x_code0", align_bytes=64, offset=3968), None]
+
+        def gather_x(a, half):
+            nc.vector.tensor_copy(
+                x_code[half][:, a, :],
+                x_w[:].bitcast(U32).indirect(piece(x_lists[a], half * HALF_S, HALF_S)),
+            )
+
+        for a in range(3):
+            gather_d(a, 0)
+            gather_x(a, 0)
+
+        w_raw = st.tile([P, 4, N], F32, name="w_raw", align_bytes=64, offset=at_w)
+        nc.scalar.dma_start(w_raw[:], w1.rearrange("(p t) m -> p t m", t=4))
+
+        ds = [sb.tile([P, S if u < 2 else 2 * S], F32, name="ds%d" % u, align_bytes=64) for u in range(4)]
+        ds2 = [sb.tile([P, S if u < 2 else 2 * S], F32, name="dn%d" % u, align_bytes=64) for u in range(4)]
+
+        def product(u, half, acc):
+            cols = slice((u % 2) * P, (u % 2 + 1) * P)
+            for a in range(3):
+                nc.tensor.matmul_mx(
+                    out=acc,
+                    lhsT=d_code[u // 2][:, a, cols].bitcast(FP8X4),
+                    lhsT_scale=d_scale[u // 2][a][:, cols],
+                    rhs=x_code[half][:, a, :].bitcast(FP8X4),
+                    rhs_scale=x_scale[half][a],
+                    start=(a == 0),
+                    stop=(a == 2),
+                )
+
+        def scatter(u, hs, start, count):
+            nc.scalar.activation(ds[u][:].indirect(piece(l_n1, start, count)), hs[:], COPY)
+            nc.scalar.activation(ds2[u][:].indirect(piece(l_n2, start, count)), hs[:], COPY, scale=-1.0)
+
+        for u in range(2):
+            acc = ps.tile([P, HALF_S], F32, name="acc%d0" % u, tag="bank%d" % u)
+            product(u, 0, acc[:])
+            hs = sb.tile([P, HALF_S], F32, name="h%d0" % u)
+            nc.scalar.activation(hs[:], acc[:], COPY, scale=gain[:, u : u + 1])
+            scatter(u, hs, 0, HALF_S)
+
+        x_scale[1] = gather_bytes(1, x_parts(1), "got1")
+        x_code[1] = st.tile([P, 3, HALF_S], U32, name="x_code1", align_bytes=64, offset=5504)
+        for a in range(3):
+            gather_x(a, 1)
+        d_scale[1] = gather_bytes(2, d_parts(1), "got2")
+
+        for u in range(2):
+            acc = ps.tile([P, HALF_S], F32, name="acc%d1" % u, tag="bank%d" % (2 + u))
+            product(u, 1, acc[:])
+            hs = sb.tile([P, HALF_S], F32, name="h%d1" % u)
+            nc.vector.tensor_scalar(hs[:], acc[:], gain[:, u : u + 1], None, MULT)
+            scatter(u, hs, HALF_S, HALF_S)
+
+        d_code[1] = st.tile([P, 3, HALF_H], U32, name="d_code1", align_bytes=64, offset=0)
+        for a in range(3):
+            gather_d(a, 1)
+
+        for u in range(2, 4):
+            acc = ps.tile([P, S], F32, name="acc%d" % u, tag="bank%d" % (u - 2))
+            for half in range(2):
+                product(u, half, acc[:, half * HALF_S : (half + 1) * HALF_S])
+            hs = sb.tile([P, S], F32, name="h%d" % u)
+            nc.vector.tensor_scalar(hs[:], acc[:], gain[:, u : u + 1], None, MULT)
+            scatter(u, hs, 0, S)
+
+        w_bf = st.tile([P, N, 4], BF16, name="w_bf", align_bytes=64, offset=0)
+        nc.vector.tensor_copy(
+            w_bf[:].rearrange("p (c i) t -> p c t i", i=4), w_raw[:].rearrange("p t (c i) -> p c t i", i=4)
+        )
+        w_code = sb.tile([P, N], U32, name="w_code", align_bytes=64)
+        w_scale = sb.tile([P, N], U8, name="w_scale", align_bytes=64)
+        nc.vector.quantize_mx(out=w_code[:].bitcast(FP8X4), scales=w_scale[:], in_=w_bf[:].rearrange("p m t -> p (m t)"))
+
+        z_t = [st.tile([P, H], BF16, name="z_t%d" % half, align_bytes=64, offset=at_w + 2 * H * half) for half in range(2)]
+        for u in range(4):
+            for half in range(2):
+                cols = slice(half * HALF_S, (half + 1) * HALF_S)
+                acc = ps.tile([P, P], F32, name="zt%d%d" % (u, half), tag="bank%d" % half)
+                nc.tensor.matmul(acc[:], ds[u][:, cols], ident[:], start=True, stop=False, is_transpose=True)
+                nc.tensor.matmul(acc[:], ds2[u][:, cols], ident[:], start=False, stop=True, is_transpose=True)
+                dst = z_t[half][:].rearrange("j (a p e) -> j a p e", a=2, e=2)[:, :, 32 * u : 32 * (u + 1), :]
+                src = acc[:].rearrange("j (p a e) -> j a p e", a=2, e=2)
+                if u == 3 and half == 1:
+                    nc.scalar.copy(dst, src)
+                else:
+                    nc.vector.tensor_copy(dst, src)
+
+        z_code, z_scale = [], []
+        for half in range(2):
+            acc = ps.tile([P, 2, P], F32, name="zb%d" % half, tag="bank%d" % (2 + half))
+            words = z_t[half][:].bitcast(F32)
+            for a in range(2):
+                nc.tensor.transpose(acc[:, a, :], words[:, a * P : (a + 1) * P], ident[:])
+            z_in = sb.tile([P, 4 * HALF_S], BF16, name="z_in%d" % half, align_bytes=64)
+            dst = z_in[:].bitcast(F32).rearrange("p (j a) -> p j a", a=2)
+            src = acc[:].rearrange("p a j -> p j a")
+            if half == 1:
+                nc.scalar.copy(dst, src)
+            else:
+                nc.vector.tensor_copy(dst, src)
+            zc = sb.tile([P, HALF_S], U32, name="z_code%d" % half, align_bytes=64)
+            zs = sb.tile([P, HALF_S], U8, name="z_scale%d" % half, align_bytes=64)
+            nc.vector.quantize_mx(out=zc[:].bitcast(FP8X4), scales=zs[:], in_=z_in[:])
+            z_code.append(zc)
+            z_scale.append(zs)
+
+        for m in range(4):
+            cols = slice(m * P, (m + 1) * P)
+            acc = ps.tile([P, S], F32, name="h2p%d" % m, tag="bank%d" % (4 + m))
+            for half in range(2):
+                nc.tensor.matmul_mx(
+                    out=acc[:, half * HALF_S : (half + 1) * HALF_S],
+                    lhsT=w_code[:, cols].bitcast(FP8X4),
+                    lhsT_scale=w_scale[:, cols],
+                    rhs=z_code[half][:].bitcast(FP8X4),
+                    rhs_scale=z_scale[half][:],
+                    start=True,
+                    stop=True,
+                )
+            h2 = sb.tile([P, S], F32, name="h2_%d" % m, align_bytes=64)
+            nc.vector.tensor_copy(h2[:], acc[:])
+            pa = sb.tile([P, W], F32, name="pa%d" % m)
+            pb = sb.tile([P, W], F32, name="pb%d" % m)
+            nc.scalar.activation(pa[:], h2[:].indirect(l_n3[:]), COPY)
+            nc.scalar.activation(pb[:], h2[:].indirect(l_n4[:]), COPY)
+            sm = sb.tile([P, W], F32, name="sm%d" % m)
+            df = sb.tile([P, W], F32, name="df%d" % m)
+            nc.vector.tensor_tensor(sm[:], pa[:], pb[:], ADD)
+            nc.vector.tensor_tensor(df[:], pa[:], pb[:], SUB)
+            res = sb.tile([P, S], F32, name="res%d" % m, align_bytes=64)
+            nc.scalar.activation(res[:].indirect(l_n3[:]), sm[:], COPY, scale=0.75)
+            nc.scalar.activation(res[:].indirect(l_n4[:]), df[:], COPY)
+            nc.sync.dma_start(out[cols, :], res[:])

@@ -33,6 +33,8 @@ def tile_picked_mtthznsndsubhaar_none_p_kernel(
         st = ctx.enter_context(tc.tile_pool(name="st", bufs=1))
         ps = ctx.enter_context(tc.psum_pool(name="ps", bufs=1))
 
+        at_w = 8128
+
         def load_list(name, ap):
             t = lists.tile(list(ap.shape), U16, name=name)
             nc.sync.dma_start(t[:], ap)
@@ -45,26 +47,26 @@ def tile_picked_mtthznsndsubhaar_none_p_kernel(
         x_sc = [st.tile([P, T], U8, name="x_sc0", align_bytes=64, offset=3008), sb.tile([P, T], U8, name="x_sc1", align_bytes=64)]
         d_w = sb.tile([P, G], I32, name="d_w", align_bytes=64)
         x_w = sb.tile([P, T], I32, name="x_w", align_bytes=64)
-        nc.gpsimd.dma_start(d_w[:], d_words[0].rearrange("p n t -> p (n t)").bitcast(I32))
-        nc.gpsimd.dma_start(x_w[:], x_words[0].rearrange("p n t -> p (n t)").bitcast(I32))
-        nc.sync.dma_start(d_sc[:].bitcast(I32), d_scales[0].bitcast(I32).unsqueeze(1).to_broadcast([16, 8, G // 4]))
-        l_k1 = load_list("l_k1", k1)
         nc.sync.dma_start(x_sc[0][:].bitcast(I32), x_scales[0].bitcast(I32).unsqueeze(1).to_broadcast([16, 8, T // 4]))
         l_offs = load_list("l_offs", offs)
-        l_k2 = load_list("l_k2", k2)
         l_two = load_list("l_two", two)
+        nc.sync.dma_start(d_sc[:].bitcast(I32), d_scales[0].bitcast(I32).unsqueeze(1).to_broadcast([16, 8, G // 4]))
+        l_k1 = load_list("l_k1", k1)
+        l_k2 = load_list("l_k2", k2)
         l_k3 = load_list("l_k3", k3)
+        nc.sync.dma_start(d_w[:], d_words[0].rearrange("p n t -> p (n t)").bitcast(I32))
         l_hz = load_list("l_hz", hz)
         d_lists = (l_k1, l_k2, l_k3)
         x_lists = (l_offs, l_two, l_hz)
 
-        gn_raw = sb.tile([P, 4], F32, name="gn_raw")
-        with nc.allow_non_contiguous_dma(reason="one gain a partition and row tile"):
-            nc.sync.dma_start(gn_raw[:], gn.rearrange("(u p) o -> p (u o)", p=P))
         l_n1 = load_list("l_n1", n1)
         l_n2 = load_list("l_n2", n2)
         l_n3 = load_list("l_n3", n3)
         l_n4 = load_list("l_n4", n4)
+        gn_raw = sb.tile([P, 4], F32, name="gn_raw")
+        with nc.allow_non_contiguous_dma(reason="one gain a partition and row tile"):
+            nc.sync.dma_start(gn_raw[:], gn.rearrange("(u p) o -> p (u o)", p=P))
+        nc.sync.dma_start(x_w[:], x_words[0].rearrange("p n t -> p (n t)").bitcast(I32))
         nc.sync.dma_start(x_sc[1][:].bitcast(I32), x_scales[0].bitcast(I32).unsqueeze(1).to_broadcast([16, 8, T // 4]))
         gain = sb.tile([P, 4], F32, name="gain")
         nc.scalar.activation(gain[:], gn_raw[:], COPY, scale=0.0625)
@@ -79,10 +81,9 @@ def tile_picked_mtthznsndsubhaar_none_p_kernel(
         make_identity(nc, ident[:])
 
         at_got = (6976, 7040, 7424)
-        at_w = 8192
 
         def gather_bytes(n, parts, tag):
-            got = st.tile([P, widths[n] + (128 if n == 0 else 0)], U8, name="got%d" % n, align_bytes=64, offset=at_got[n])
+            got = st.tile([P, widths[n]], U8, name="got%d" % n, align_bytes=64, offset=at_got[n])
             at, res = 0, []
             for src, lst, count in parts:
                 nc.vector.tensor_copy(got[:, at : at + count], src[:].indirect(lst))
@@ -98,12 +99,9 @@ def tile_picked_mtthznsndsubhaar_none_p_kernel(
         def x_parts(half):
             return [(x_sc[half], piece(l, half * HALF_S, HALF_S), HALF_S) for l in x_lists]
 
-        mixed = []
-        for a, b in zip(d_parts(0), x_parts(0)):
-            mixed.extend([a, b])
-        sc0 = gather_bytes(0, mixed, "got0")
-        d_scale = [sc0[0::2], None]
-        x_scale = [sc0[1::2], None]
+        sc0 = gather_bytes(0, x_parts(0)[:2] + d_parts(0) + x_parts(0)[2:], "got0")
+        d_scale = [sc0[2:5], None]
+        x_scale = [sc0[:2] + sc0[5:], None]
 
         d_code = [st.tile([P, 3, HALF_H], U32, name="d_code0", align_bytes=64, offset=0), None]
 
@@ -120,12 +118,12 @@ def tile_picked_mtthznsndsubhaar_none_p_kernel(
                 x_w[:].bitcast(U32).indirect(piece(x_lists[a], half * HALF_S, HALF_S)),
             )
 
-        for a in range(3):
-            gather_d(a, 0)
-            gather_x(a, 0)
+        for group in ((0, 1), (2,)):
+            for a in group:
+                gather_d(a, 0)
+            for a in group:
+                gather_x(a, 0)
 
-        w_raw = st.tile([P, 4, N], F32, name="w_raw", align_bytes=64, offset=at_w)
-        nc.scalar.dma_start(w_raw[:], w1.rearrange("(p t) m -> p t m", t=4))
 
         ds = [sb.tile([P, S if u < 2 else 2 * S], F32, name="ds%d" % u, align_bytes=64) for u in range(4)]
         ds2 = [sb.tile([P, S if u < 2 else 2 * S], F32, name="dn%d" % u, align_bytes=64) for u in range(4)]
@@ -159,6 +157,8 @@ def tile_picked_mtthznsndsubhaar_none_p_kernel(
         for a in range(3):
             gather_x(a, 1)
         d_scale[1] = gather_bytes(2, d_parts(1), "got2")
+        w_raw = st.tile([P, 4, N], F32, name="w_raw", align_bytes=64, offset=at_w)
+        nc.sync.dma_start(w_raw[:], w1.rearrange("(p t) m -> p t m", t=4))
 
         for u in range(2):
             acc = ps.tile([P, HALF_S], F32, name="acc%d1" % u, tag="bank%d" % (2 + u))
@@ -187,7 +187,7 @@ def tile_picked_mtthznsndsubhaar_none_p_kernel(
         w_scale = sb.tile([P, N], U8, name="w_scale", align_bytes=64)
         nc.vector.quantize_mx(out=w_code[:].bitcast(FP8X4), scales=w_scale[:], in_=w_bf[:].rearrange("p m t -> p (m t)"))
 
-        z_t = [st.tile([P, H], BF16, name="z_t%d" % half, align_bytes=64, offset=at_w + 2 * H * half) for half in range(2)]
+        z_t = [st.tile([P, H], BF16, name="z_t%d" % half, align_bytes=64, offset=at_w + 64 + 2 * H * half) for half in range(2)]
         for u in range(4):
             for half in range(2):
                 cols = slice(half * HALF_S, (half + 1) * HALF_S)
@@ -210,22 +210,25 @@ def tile_picked_mtthznsndsubhaar_none_p_kernel(
             z_in = sb.tile([P, 4 * HALF_S], BF16, name="z_in%d" % half, align_bytes=64)
             dst = z_in[:].bitcast(F32).rearrange("p (j a) -> p j a", a=2)
             src = acc[:].rearrange("p a j -> p j a")
-            if half == 1:
-                nc.scalar.copy(dst, src)
-            else:
-                nc.vector.tensor_copy(dst, src)
+            nc.scalar.copy(dst, src)
             zc = sb.tile([P, HALF_S], U32, name="z_code%d" % half, align_bytes=64)
             zs = sb.tile([P, HALF_S], U8, name="z_scale%d" % half, align_bytes=64)
             nc.vector.quantize_mx(out=zc[:].bitcast(FP8X4), scales=zs[:], in_=z_in[:])
             z_code.append(zc)
             z_scale.append(zs)
 
+        pa, pb = [], []
         for m in range(4):
             cols = slice(m * P, (m + 1) * P)
             acc = ps.tile([P, S], F32, name="h2p%d" % m, tag="bank%d" % (4 + m))
+            h2 = sb.tile([P, S], F32, name="h2_%d" % m, align_bytes=64)
+            parts = [acc[:, :HALF_S], acc[:, HALF_S:]]
+            if m == 0:
+                side = ps.tile([P, HALF_S], F32, name="h2side", tag="bank0")
+                parts[0] = side[:]
             for half in range(2):
                 nc.tensor.matmul_mx(
-                    out=acc[:, half * HALF_S : (half + 1) * HALF_S],
+                    out=parts[half],
                     lhsT=w_code[:, cols].bitcast(FP8X4),
                     lhsT_scale=w_scale[:, cols],
                     rhs=z_code[half][:].bitcast(FP8X4),
@@ -233,17 +236,25 @@ def tile_picked_mtthznsndsubhaar_none_p_kernel(
                     start=True,
                     stop=True,
                 )
-            h2 = sb.tile([P, S], F32, name="h2_%d" % m, align_bytes=64)
-            nc.vector.tensor_copy(h2[:], acc[:])
-            pa = sb.tile([P, W], F32, name="pa%d" % m)
-            pb = sb.tile([P, W], F32, name="pb%d" % m)
-            nc.scalar.activation(pa[:], h2[:].indirect(l_n3[:]), COPY)
-            nc.scalar.activation(pb[:], h2[:].indirect(l_n4[:]), COPY)
-            sm = sb.tile([P, W], F32, name="sm%d" % m)
-            df = sb.tile([P, W], F32, name="df%d" % m)
-            nc.vector.tensor_tensor(sm[:], pa[:], pb[:], ADD)
-            nc.vector.tensor_tensor(df[:], pa[:], pb[:], SUB)
-            res = sb.tile([P, S], F32, name="res%d" % m, align_bytes=64)
-            nc.scalar.activation(res[:].indirect(l_n3[:]), sm[:], COPY, scale=0.75)
-            nc.scalar.activation(res[:].indirect(l_n4[:]), df[:], COPY)
-            nc.sync.dma_start(out[cols, :], res[:])
+            if m == 0:
+                for half in range(2):
+                    nc.scalar.copy(h2[:, half * HALF_S : (half + 1) * HALF_S], parts[half])
+            else:
+                nc.vector.tensor_copy(h2[:], acc[:])
+            pa.append(sb.tile([P, W], F32, name="pa%d" % m))
+            pb.append(sb.tile([P, W], F32, name="pb%d" % m))
+            nc.scalar.activation(pa[m][:], h2[:].indirect(l_n3[:]), COPY)
+            nc.scalar.activation(pb[m][:], h2[:].indirect(l_n4[:]), COPY)
+        sm, df, res = [], [], []
+        for m in range(4):
+            sm.append(sb.tile([P, W], F32, name="sm%d" % m))
+            df.append(sb.tile([P, W], F32, name="df%d" % m))
+            res.append(sb.tile([P, S], F32, name="res%d" % m, align_bytes=64))
+            nc.vector.tensor_tensor(sm[m][:], pa[m][:], pb[m][:], ADD)
+            nc.vector.tensor_tensor(df[m][:], pa[m][:], pb[m][:], SUB)
+        for pair in range(2):
+            for m in (2 * pair, 2 * pair + 1):
+                nc.scalar.activation(res[m][:].indirect(l_n3[:]), sm[m][:], COPY, scale=0.75)
+            for m in (2 * pair, 2 * pair + 1):
+                nc.scalar.activation(res[m][:].indirect(l_n4[:]), df[m][:], COPY)
+                nc.sync.dma_start(out[m * P : (m + 1) * P, :], res[m][:])

@@ -47,10 +47,13 @@ def tile_picked_mtthznsndsubhaar_none_p_kernel(
         x_sc = [st.tile([P, T], U8, name="x_sc0", align_bytes=64, offset=3008), sb.tile([P, T], U8, name="x_sc1", align_bytes=64)]
         d_w = sb.tile([P, G], I32, name="d_w", align_bytes=64)
         x_w = sb.tile([P, T], I32, name="x_w", align_bytes=64)
-        nc.sync.dma_start(x_sc[0][:].bitcast(I32), x_scales[0].bitcast(I32).unsqueeze(1).to_broadcast([16, 8, T // 4]))
+        nc.gpsimd.memset(x_sc[0][:].bitcast(I32), 0)
+        nc.vector.memset(d_sc[:].bitcast(I32), 0)
+        nc.vector.memset(x_sc[1][:].bitcast(I32), 0)
+        nc.sync.dma_start(x_sc[0][0:P:8, :].bitcast(I32), x_scales[0].bitcast(I32))
         l_offs = load_list("l_offs", offs)
         l_two = load_list("l_two", two)
-        nc.sync.dma_start(d_sc[:].bitcast(I32), d_scales[0].bitcast(I32).unsqueeze(1).to_broadcast([16, 8, G // 4]))
+        nc.sync.dma_start(d_sc[0:P:8, :].bitcast(I32), d_scales[0].bitcast(I32))
         l_k1 = load_list("l_k1", k1)
         l_k2 = load_list("l_k2", k2)
         l_k3 = load_list("l_k3", k3)
@@ -65,9 +68,9 @@ def tile_picked_mtthznsndsubhaar_none_p_kernel(
         l_n4 = load_list("l_n4", n4)
         gn_raw = sb.tile([P, 4], F32, name="gn_raw")
         with nc.allow_non_contiguous_dma(reason="one gain a partition and row tile"):
-            nc.sync.dma_start(gn_raw[:], gn.rearrange("(u p) o -> p (u o)", p=P))
+            nc.gpsimd.dma_start(gn_raw[:], gn.rearrange("(u p) o -> p (u o)", p=P))
         nc.sync.dma_start(x_w[:], x_words[0].rearrange("p n t -> p (n t)").bitcast(I32))
-        nc.sync.dma_start(x_sc[1][:].bitcast(I32), x_scales[0].bitcast(I32).unsqueeze(1).to_broadcast([16, 8, T // 4]))
+        nc.sync.dma_start(x_sc[1][0:P:8, :].bitcast(I32), x_scales[0].bitcast(I32))
         gain = sb.tile([P, 4], F32, name="gain")
         nc.scalar.activation(gain[:], gn_raw[:], COPY, scale=0.0625)
 

from contextlib import ExitStack

import concourse.mybir as mybir
from concourse.masks import make_identity

K, T, S, N, G, H, W = 512, 1024, 256, 512, 2048, 512, 128
FLOPS = 3 * 2 * K * H * S + 2 * H * N * S

F32 = mybir.dt.float32
BF16 = mybir.dt.bfloat16
I32 = mybir.dt.int32
U32 = mybir.dt.uint32
U16 = mybir.dt.uint16
U8 = mybir.dt.uint8
FP8X4 = mybir.dt.float8_e4m3fn_x4
COPY = mybir.ActivationFunctionType.Copy
ADD = mybir.AluOpType.add
SUB = mybir.AluOpType.subtract
MULT = mybir.AluOpType.mult

P = 128
HALF_S = S // 2
HALF_H = H // 2


def tile_picked_mtthznsndsubhaar_none_p_kernel(
    tc, x_words, x_scales, d_words, d_scales, gn, w1, offs, k1, two, k2, hz, k3, n1, n2, n3, n4, out
):
    nc = tc.nc
    with ExitStack() as ctx:
        lists = ctx.enter_context(tc.tile_pool(name="lists", bufs=1))
        sb = ctx.enter_context(tc.tile_pool(name="sb", bufs=1))
        st = ctx.enter_context(tc.tile_pool(name="st", bufs=1))
        ps = ctx.enter_context(tc.psum_pool(name="ps", bufs=1))

        at_w = 8128

        def load_list(name, ap):
            t = lists.tile(list(ap.shape), U16, name=name)
            nc.sync.dma_start(t[:], ap)
            return t

        def piece(lst, start, count):
            return lst[:, start // 16 : (start + count) // 16]

        d_sc = sb.tile([P, G], U8, name="d_sc", align_bytes=64)
        x_sc = [st.tile([P, T], U8, name="x_sc0", align_bytes=64, offset=3008), sb.tile([P, T], U8, name="x_sc1", align_bytes=64)]
        d_w = sb.tile([P, G], I32, name="d_w", align_bytes=64)
        x_w = sb.tile([P, T], I32, name="x_w", align_bytes=64)
        nc.gpsimd.memset(x_sc[0][:].bitcast(I32), 0)
        nc.vector.memset(d_sc[:].bitcast(I32), 0)
        nc.vector.memset(x_sc[1][:].bitcast(I32), 0)
        nc.sync.dma_start(x_sc[0][0:P:8, :].bitcast(I32), x_scales[0].bitcast(I32))
        l_offs = load_list("l_offs", offs)
        l_two = load_list("l_two", two)
        nc.sync.dma_start(d_sc[0:P:8, :].bitcast(I32), d_scales[0].bitcast(I32))
        l_k1 = load_list("l_k1", k1)
        l_k2 = load_list("l_k2", k2)
        l_k3 = load_list("l_k3", k3)
        nc.sync.dma_start(d_w[:], d_words[0].rearrange("p n t -> p (n t)").bitcast(I32))
        l_hz = load_list("l_hz", hz)
        d_lists = (l_k1, l_k2, l_k3)
        x_lists = (l_offs, l_two, l_hz)

        l_n1 = load_list("l_n1", n1)
        l_n2 = load_list("l_n2", n2)
        l_n3 = load_list("l_n3", n3)
        l_n4 = load_list("l_n4", n4)
        gn_raw = sb.tile([P, 4], F32, name="gn_raw")
        with nc.allow_non_contiguous_dma(reason="one gain a partition and row tile"):
            nc.gpsimd.dma_start(gn_raw[:], gn.rearrange("(u p) o -> p (u o)", p=P))
        nc.sync.dma_start(x_w[:], x_words[0].rearrange("p n t -> p (n t)").bitcast(I32))
        nc.sync.dma_start(x_sc[1][0:P:8, :].bitcast(I32), x_scales[0].bitcast(I32))
        gain = sb.tile([P, 4], F32, name="gain")
        nc.scalar.activation(gain[:], gn_raw[:], COPY, scale=0.0625)

        widths = (3 * HALF_H + 3 * HALF_S, 3 * HALF_S, 3 * HALF_H)
        planes = []
        for n, width in enumerate(widths):
            pl = sb.tile([P, width], U8, name="plane%d" % n, align_bytes=64)
            nc.gpsimd.memset(pl[:].bitcast(I32), 0)
            planes.append(pl)
        ident = sb.tile([P, P], F32, name="ident", align_bytes=64)
        make_identity(nc, ident[:])

        at_got = (6976, 7040, 7424)

        def gather_bytes(n, parts, tag):
            got = st.tile([P, widths[n]], U8, name="got%d" % n, align_bytes=64, offset=at_got[n])
            at, res = 0, []
            for src, lst, count in parts:
                nc.vector.tensor_copy(got[:, at : at + count], src[:].indirect(lst))
                res.append(planes[n][:, at : at + count])
                at = at + count
            for r in range(4):
                nc.sync.dma_start(planes[n][r:P:32, :].bitcast(I32), got[8 * r : P : 32, : widths[n]].bitcast(I32))
            return res

        def d_parts(half):
            return [(d_sc, piece(l, half * HALF_H, HALF_H), HALF_H) for l in d_lists]

        def x_parts(half):
            return [(x_sc[half], piece(l, half * HALF_S, HALF_S), HALF_S) for l in x_lists]

        sc0 = gather_bytes(0, x_parts(0)[:2] + d_parts(0) + x_parts(0)[2:], "got0")
        d_scale = [sc0[2:5], None]
        x_scale = [sc0[:2] + sc0[5:], None]

        d_code = [st.tile([P, 3, HALF_H], U32, name="d_code0", align_bytes=64, offset=0), None]

        def gather_d(a, half):
            nc.vector.tensor_copy(
                d_code[half][:, a, :], d_w[:].bitcast(U32).indirect(piece(d_lists[a], half * HALF_H, HALF_H))
            )

        x_code = [st.tile([P, 3, HALF_S], U32, name="x_code0", align_bytes=64, offset=3968), None]

        def gather_x(a, half):
            nc.vector.tensor_copy(
                x_code[half][:, a, :],
                x_w[:].bitcast(U32).indirect(piece(x_lists[a], half * HALF_S, HALF_S)),
            )

        for group in ((0, 1), (2,)):
            for a in group:
                gather_d(a, 0)
            for a in group:
                gather_x(a, 0)


        ds = [sb.tile([P, S if u < 2 else 2 * S], F32, name="ds%d" % u, align_bytes=64) for u in range(4)]
        ds2 = [sb.tile([P, S if u < 2 else 2 * S], F32, name="dn%d" % u, align_bytes=64) for u in range(4)]

        def product(u, half, acc):
            cols = slice((u % 2) * P, (u % 2 + 1) * P)
            for a in range(3):
                nc.tensor.matmul_mx(
                    out=acc,
                    lhsT=d_code[u // 2][:, a, cols].bitcast(FP8X4),
                    lhsT_scale=d_scale[u // 2][a][:, cols],
                    rhs=x_code[half][:, a, :].bitcast(FP8X4),
                    rhs_scale=x_scale[half][a],
                    start=(a == 0),
                    stop=(a == 2),
                )

        def scatter(u, hs, start, count):
            nc.scalar.activation(ds[u][:].indirect(piece(l_n1, start, count)), hs[:], COPY)
            nc.scalar.activation(ds2[u][:].indirect(piece(l_n2, start, count)), hs[:], COPY, scale=-1.0)

        for u in range(2):
            acc = ps.tile([P, HALF_S], F32, name="acc%d0" % u, tag="bank%d" % u)
            product(u, 0, acc[:])
            hs = sb.tile([P, HALF_S], F32, name="h%d0" % u)
            nc.scalar.activation(hs[:], acc[:], COPY, scale=gain[:, u : u + 1])
            scatter(u, hs, 0, HALF_S)

        x_scale[1] = gather_bytes(1, x_parts(1), "got1")
        x_code[1] = st.tile([P, 3, HALF_S], U32, name="x_code1", align_bytes=64, offset=5504)
        for a in range(3):
            gather_x(a, 1)
        d_scale[1] = gather_bytes(2, d_parts(1), "got2")
        w_raw = st.tile([P, 4, N], F32, name="w_raw", align_bytes=64, offset=at_w)
        nc.sync.dma_start(w_raw[:], w1.rearrange("(p t) m -> p t m", t=4))

        for u in range(2):
            acc = ps.tile([P, HALF_S], F32, name="acc%d1" % u, tag="bank%d" % (2 + u))
            product(u, 1, acc[:])
            hs = sb.tile([P, HALF_S], F32, name="h%d1" % u)
            nc.vector.tensor_scalar(hs[:], acc[:], gain[:, u : u + 1], None, MULT)
            scatter(u, hs, HALF_S, HALF_S)

        d_code[1] = st.tile([P, 3, HALF_H], U32, name="d_code1", align_bytes=64, offset=0)
        for a in range(3):
            gather_d(a, 1)

        for u in range(2, 4):
            acc = ps.tile([P, S], F32, name="acc%d" % u, tag="bank%d" % (u - 2))
            for half in range(2):
                product(u, half, acc[:, half * HALF_S : (half + 1) * HALF_S])
            hs = sb.tile([P, S], F32, name="h%d" % u)
            nc.vector.tensor_scalar(hs[:], acc[:], gain[:, u : u + 1], None, MULT)
            scatter(u, hs, 0, S)

        w_bf = st.tile([P, N, 4], BF16, name="w_bf", align_bytes=64, offset=0)
        nc.vector.tensor_copy(
            w_bf[:].rearrange("p (c i) t -> p c t i", i=4), w_raw[:].rearrange("p t (c i) -> p c t i", i=4)
        )
        w_code = sb.tile([P, N], U32, name="w_code", align_bytes=64)
        w_scale = sb.tile([P, N], U8, name="w_scale", align_bytes=64)
        nc.vector.quantize_mx(out=w_code[:].bitcast(FP8X4), scales=w_scale[:], in_=w_bf[:].rearrange("p m t -> p (m t)"))

        z_t = [st.tile([P, H], BF16, name="z_t%d" % half, align_bytes=64, offset=at_w + 64 + 2 * H * half) for half in range(2)]
        for u in range(4):
            for half in range(2):
                cols = slice(half * HALF_S, (half + 1) * HALF_S)
                acc = ps.tile([P, P], F32, name="zt%d%d" % (u, half), tag="bank%d" % half)
                nc.tensor.matmul(acc[:], ds[u][:, cols], ident[:], start=True, stop=False, is_transpose=True)
                nc.tensor.matmul(acc[:], ds2[u][:, cols], ident[:], start=False, stop=True, is_transpose=True)
                dst = z_t[half][:].rearrange("j (a p e) -> j a p e", a=2, e=2)[:, :, 32 * u : 32 * (u + 1), :]
                src = acc[:].rearrange("j (p a e) -> j a p e", a=2, e=2)
                if u == 3 and half == 1:
                    nc.scalar.copy(dst, src)
                else:
                    nc.vector.tensor_copy(dst, src)

        z_code, z_scale = [], []
        for half in range(2):
            acc = ps.tile([P, 2, P], F32, name="zb%d" % half, tag="bank%d" % (2 + half))
            words = z_t[half][:].bitcast(F32)
            for a in range(2):
                nc.tensor.transpose(acc[:, a, :], words[:, a * P : (a + 1) * P], ident[:])
            z_in = sb.tile([P, 4 * HALF_S], BF16, name="z_in%d" % half, align_bytes=64)
            dst = z_in[:].bitcast(F32).rearrange("p (j a) -> p j a", a=2)
            src = acc[:].rearrange("p a j -> p j a")
            nc.scalar.copy(dst, src)
            zc = sb.tile([P, HALF_S], U32, name="z_code%d" % half, align_bytes=64)
            zs = sb.tile([P, HALF_S], U8, name="z_scale%d" % half, align_bytes=64)
            nc.vector.quantize_mx(out=zc[:].bitcast(FP8X4), scales=zs[:], in_=z_in[:])
            z_code.append(zc)
            z_scale.append(zs)

        pa, pb = [], []
        for m in range(4):
            cols = slice(m * P, (m + 1) * P)
            acc = ps.tile([P, S], F32, name="h2p%d" % m, tag="bank%d" % (4 + m))
            h2 = sb.tile([P, S], F32, name="h2_%d" % m, align_bytes=64)
            parts = [acc[:, :HALF_S], acc[:, HALF_S:]]
            if m == 0:
                side = ps.tile([P, HALF_S], F32, name="h2side", tag="bank0")
                parts[0] = side[:]
            for half in range(2):
                nc.tensor.matmul_mx(
                    out=parts[half],
                    lhsT=w_code[:, cols].bitcast(FP8X4),
                    lhsT_scale=w_scale[:, cols],
                    rhs=z_code[half][:].bitcast(FP8X4),
                    rhs_scale=z_scale[half][:],
                    start=True,
                    stop=True,
                )
            if m == 0:
                for half in range(2):
                    nc.scalar.copy(h2[:, half * HALF_S : (half + 1) * HALF_S], parts[half])
            else:
                nc.vector.tensor_copy(h2[:], acc[:])
            pa.append(sb.tile([P, W], F32, name="pa%d" % m))
            pb.append(sb.tile([P, W], F32, name="pb%d" % m))
            nc.scalar.activation(pa[m][:], h2[:].indirect(l_n3[:]), COPY)
            nc.scalar.activation(pb[m][:], h2[:].indirect(l_n4[:]), COPY)
        sm, df, res = [], [], []
        for m in range(4):
            sm.append(sb.tile([P, W], F32, name="sm%d" % m))
            df.append(sb.tile([P, W], F32, name="df%d" % m))
            res.append(sb.tile([P, S], F32, name="res%d" % m, align_bytes=64))
            nc.vector.tensor_tensor(sm[m][:], pa[m][:], pb[m][:], ADD)
            nc.vector.tensor_tensor(df[m][:], pa[m][:], pb[m][:], SUB)
        for pair in range(2):
            for m in (2 * pair, 2 * pair + 1):
                nc.scalar.activation(res[m][:].indirect(l_n3[:]), sm[m][:], COPY, scale=0.75)
            for m in (2 * pair, 2 * pair + 1):
                nc.scalar.activation(res[m][:].indirect(l_n4[:]), df[m][:], COPY)
                nc.sync.dma_start(out[m * P : (m + 1) * P, :], res[m][:])
